import numpy as np
import ml_dtypes


def mxq(x, axis, fmt="e4m3"):
    dtype, down = {"e4m3": (ml_dtypes.float8_e4m3fn, 7), "e5m2": (ml_dtypes.float8_e5m2, 14)}[fmt]
    v = np.moveaxis(np.asarray(x, np.float32).astype(ml_dtypes.bfloat16).astype(np.float64), axis, -1)
    blocks = v.reshape(v.shape[:-1] + (-1, 32))
    amax = np.abs(blocks).max(-1, keepdims=True)
    byte = np.maximum(np.where(amax > 0, np.frexp(amax)[1] - 1 + 127, 0) - down, 1)
    scale = np.exp2(byte - 127.0)
    codes = (blocks / scale).astype(np.float32).astype(dtype).astype(np.float64)
    return np.moveaxis((codes * scale).reshape(v.shape), -1, axis)


WIDE = False


def mx_kscale(k):
    if not WIDE:
        return np.ones(k)
    levels = np.array([10, -10, 5, -5, 0])
    if k % 512:
        return np.exp2(np.random.permutation(np.resize(levels, k // 32))).repeat(32)
    a = np.empty((k // 512, 16))
    for p in range(k // 512):
        a[p, :8] = np.random.permutation(np.resize(levels, 8))
        for g in range(8):
            far = levels[np.abs(levels - a[p, g]) >= 10]
            a[p, g + 8] = far[np.random.randint(len(far))]
    return np.exp2(a.ravel()).repeat(32)


def f64(x):
    return np.asarray(x).astype(np.float64)


def striped(idx):
    return np.tile(idx.reshape(-1, 16).T, (8, 1)).astype(np.uint16)


def unstriped(offs):
    return offs[:16].T.reshape(-1).astype(np.int64)


E2M1 = np.array([0.0, 0.5, 1.0, 1.5, 2.0, 3.0, 4.0, 6.0, -0.0, -0.5, -1.0, -1.5, -2.0, -3.0, -4.0, -6.0])


def pack_weight(w, fmt):
    k, n = w.shape
    w = f64(np.asarray(w, np.float32).astype(ml_dtypes.bfloat16)).reshape(k // 32, 32, n)
    amax = np.abs(w).max(1)
    if fmt == "e4m3":
        byte = np.frexp(amax)[1] - 1 + 127 - 7
    else:
        mant, ex = np.frexp(amax / 6.0)
        byte = np.where(mant > 0.5, ex, ex - 1) + 127
    byte = np.clip(np.where(amax > 0, byte, 1), 1, 254)
    scaled = (w * np.exp2(127.0 - byte)[:, None, :]).reshape(k, n).astype(np.float32)
    by_word = np.ascontiguousarray(scaled.reshape(k // 512, 128, 4, n).transpose(0, 1, 3, 2))
    if fmt == "e4m3":
        words = by_word.astype(ml_dtypes.float8_e4m3fn).view(np.uint8)
    else:
        c = by_word.astype(ml_dtypes.float4_e2m1fn).view(np.uint8) & 0xF
        words = (c[..., 0::2] | (c[..., 1::2] << 4)).reshape(k // 512, 128, 2 * n)
    return np.ascontiguousarray(words), np.ascontiguousarray(byte.astype(np.uint8).reshape(k // 512, 16, n))


def unpack_weight(words, scales, fmt):
    g, _, n = scales.shape
    words = np.ascontiguousarray(words).reshape(g, 128, n, -1)
    if fmt == "e4m3":
        vals = words.view(ml_dtypes.float8_e4m3fn).astype(np.float64)
    else:
        nib = np.empty((g, 128, n, 4), np.uint8)
        nib[..., 0::2] = words & 0xF
        nib[..., 1::2] = words >> 4
        vals = E2M1[nib]
    vals = vals * np.repeat(np.exp2(scales.astype(np.float64) - 127.0), 8, axis=1)[..., None]
    return vals.transpose(0, 1, 3, 2).reshape(g * 512, n)


def gelu(v):
    return 0.5 * v * (1.0 + np.tanh(np.sqrt(2.0 / np.pi) * (v + 0.044715 * v**3)))


def bf(x):
    return np.asarray(x, np.float32).astype(ml_dtypes.bfloat16)


def planes(Y):
    n, m = Y.shape
    b = f64(bf(Y)).reshape(n // 32, 32, m)
    amax = np.abs(b).max(1)
    byte = np.clip(np.where(amax > 0, np.frexp(amax)[1] - 1 + 127 - 7, 1), 1, 254)
    codes = (b * np.exp2(127.0 - byte)[:, None, :]).reshape(n, m).astype(np.float32).astype(ml_dtypes.float8_e4m3fn).view(np.uint8)
    words = codes.reshape(n // 512, 128, 4, m).transpose(0, 1, 3, 2)
    return np.ascontiguousarray(words), np.ascontiguousarray(byte.astype(np.uint8).reshape(n // 512, 16, m))


K, H, N, T, S, P = 1536, 1024, 512, 4096, 1024, 512

def setup_inputs():
    n = np.random.standard_normal
    s = mx_kscale(K)[:, None]
    u = mx_kscale(H)[:, None]
    tab_words, tab_scales = pack_weight(n((K, T)) * s, "e4m3")
    w4_words, w4_scales = pack_weight(n((H, N)) / np.sqrt(H) / u, "e2m1")
    w1 = 0.8 * n((K, H)) / np.sqrt(K) / s
    tilt = np.random.choice([-1.0, 1.0], H) * np.random.uniform(2.0, 5.0, H) * u[:, 0]
    mix = 8.0 * n((H, P)) * u
    tenor = np.exp(0.8 * n(N))[:, None] * np.random.uniform(0.5, 1.5, (N, P))
    return {
        "tab_words": tab_words, "tab_scales": tab_scales,
        "offs": striped(np.random.permutation(T)[:S]),
        "pos1": striped(np.random.permutation(S)[:P]),
        "pos2": striped(np.random.permutation(S)[:P]),
        "w1": w1.astype(np.float32),
        "temp": np.random.uniform(0.4, 1.6, H).astype(np.float32),
        "steep": np.random.uniform(0.6, 3.0, H).astype(np.float32),
        "thr": n(H).astype(np.float32),
        "tilt": tilt.astype(np.float32),
        "mix": mix.astype(np.float32),
        "w4_words": w4_words, "w4_scales": w4_scales,
        "tenor": tenor.astype(np.float32),
    }

def reference(tab_words, tab_scales, offs, pos1, pos2, w1, temp, steep, thr, tilt, mix, w4_words, w4_scales, tenor):
    v = unpack_weight(tab_words, tab_scales, "e4m3")[:, unstriped(offs)]
    h = mxq(f64(w1), 0, "e4m3").T @ v
    top = h.max(axis=1)
    a = np.exp(f64(temp)[:, None] * (h[:, unstriped(pos1)] - top[:, None]))
    c = 1.0 / (1.0 + np.exp(-(f64(steep)[:, None] * h[:, unstriped(pos2)] + f64(thr)[:, None])))
    z = f64(tilt)[:, None] * a + a * c * f64(mix)
    w4 = unpack_weight(w4_words, w4_scales, "e2m1")
    y = (w4.T @ mxq(z, 0, "e4m3")) * f64(tenor)
    words, scales = planes(y)
    return y, words, scales

@@ -1,0 +1,317 @@
+from contextlib import ExitStack
+
+import concourse.mybir as mybir
+
+K, H, N, T, S, M = 1536, 1024, 512, 4096, 1024, 512
+FLOPS = 2 * K * H * S + 2 * H * N * M
+
+F32 = mybir.dt.float32
+BF16 = mybir.dt.bfloat16
+I32 = mybir.dt.int32
+U32 = mybir.dt.uint32
+U16 = mybir.dt.uint16
+U8 = mybir.dt.uint8
+FP8X4 = mybir.dt.float8_e4m3fn_x4
+FP4X4 = mybir.dt.float4_e2m1fn_x4
+ACT = mybir.ActivationFunctionType
+ALU = mybir.AluOpType
+
+P = 128
+PACK = 4
+GROUP = P * PACK
+KP = K // GROUP
+RB = H // GROUP
+BANK = 512
+HALF = M // 2
+QUARTER = M // 4
+
+
+def tile_list_swap_tenor_pressure_kernel(
+    tc, tab_words, tab_scales, offs, pos1, pos2, w1, temp, steep, thr, tilt, mix,
+    w4_words, w4_scales, tenor, out_0, out_1, out_2,
+):
+    nc = tc.nc
+    with ExitStack() as ctx:
+        lists = ctx.enter_context(tc.tile_pool(name="lists", bufs=1))
+        keep = ctx.enter_context(tc.tile_pool(name="keep", bufs=1))
+        stage = ctx.enter_context(tc.tile_pool(name="stage", bufs=3))
+        ring = ctx.enter_context(tc.tile_pool(name="ring", bufs=RB * KP))
+        psum = ctx.enter_context(tc.psum_pool(name="psum", bufs=1))
+
+        idx_list = lists.tile([P, S // 16], U16, name="idx_list")
+        p1_list = lists.tile([P, M // 16], U16, name="p1_list")
+        p2_list = lists.tile([P, M // 16], U16, name="p2_list")
+
+        tab_scale = keep.tile([P, T], U8, name="tab_scale", align_bytes=64)
+        w4_scale_raw = keep.tile([P, RB, N], U8, name="w4_scale_raw", align_bytes=64)
+        w4_raw = keep.tile([P, RB, 2 * N], U8, name="w4_raw", align_bytes=64)
+        nc.vector.memset(tab_scale[:].bitcast(I32), 0)
+        nc.vector.memset(w4_scale_raw[:].rearrange("p b n -> p (b n)").bitcast(I32), 0)
+
+        tab = [keep.tile([P, T], U32, name=f"tab{a}", tag=f"big{a}", align_bytes=64) for a in range(KP)]
+
+        def load_tab(a):
+            nc.sync.dma_start(out=tab[a][:].bitcast(I32), in_=tab_words[a].rearrange("p t i -> p (t i)").bitcast(I32))
+
+        def load_w1(b, a, pieces):
+            raw = ring.tile([P, PACK, GROUP], F32, name="w1_raw", tag="rows")
+            rows = w1[a * GROUP : (a + 1) * GROUP, b * GROUP : (b + 1) * GROUP].rearrange("(p j) c -> p j c", j=PACK)
+            width = GROUP // pieces
+            for s in range(pieces):
+                cols = slice(s * width, (s + 1) * width)
+                nc.sync.dma_start(out=raw[:, :, cols], in_=rows[:, :, cols])
+            return raw
+
+        row_consts = {}
+        for name, vec in (("temp", temp), ("steep", steep), ("thr", thr), ("tilt", tilt)):
+            tile_v = keep.tile([P, RB * PACK], F32, name=f"{name}_cols")
+            nc.gpsimd.dma_start(
+                out=tile_v[:].rearrange("p (b t) -> p b t", t=PACK),
+                in_=vec.rearrange("(b p t) -> p b t", b=RB, t=PACK),
+            )
+            row_consts[name] = tile_v
+        nc.sync.dma_start(idx_list[:], offs)
+        load_tab(0)
+        scale_rows = keep.tile([P, T // 4], I32, name="scale_rows")
+        for quad in range(4):
+            nc.sync.dma_start(
+                out=scale_rows[32 * quad : 32 * quad + 4 * KP, :],
+                in_=tab_scales[:, 4 * quad : 4 * quad + 4, :].bitcast(I32),
+            )
+        w1_raw = {}
+        w1_raw[0, 0] = load_w1(0, 0, 1)
+        load_tab(1)
+        nc.sync.dma_start(out=w4_raw[:].bitcast(I32), in_=w4_words.rearrange("b p c -> p b c").bitcast(I32))
+        w1_raw[0, 1] = load_w1(0, 1, 1)
+        for quad in range(4):
+            nc.sync.dma_start(
+                out=w4_scale_raw[32 * quad : 32 * quad + 4].bitcast(I32),
+                in_=w4_scales[:, 4 * quad : 4 * quad + 4, :].rearrange("b r c -> r b c").bitcast(I32),
+            )
+        load_tab(2)
+        w1_raw[0, 2] = load_w1(0, 2, 2)
+        nc.sync.dma_start(p1_list[:], pos1)
+        nc.sync.dma_start(p2_list[:], pos2)
+
+        for quad in range(4):
+            rows = slice(32 * quad, 32 * quad + 4 * KP)
+            nc.vector.tensor_copy(out=tab_scale[rows, :].bitcast(I32), in_=scale_rows[rows, :])
+
+        w4_code = keep.tile([P, RB, 2 * N], U8, name="w4_code", align_bytes=64)
+        w4_scale = keep.tile([P, RB, N], U8, name="w4_scale", align_bytes=64)
+        for b in range(RB):
+            nc.vector.tensor_copy(
+                out=w4_code[:, b, :].rearrange("p (t q e) -> p t q e", t=PACK, e=2),
+                in_=w4_raw[:, b, :].rearrange("p (q t e) -> p t q e", t=PACK, e=2),
+            )
+        nc.vector.tensor_copy(
+            out=w4_scale[:].rearrange("p b (t q) -> p b t q", t=PACK),
+            in_=w4_scale_raw[:].rearrange("p b (q t) -> p b t q", t=PACK),
+        )
+        neg_temp = keep.tile([P, RB * PACK], F32, name="neg_temp")
+        nc.vector.tensor_scalar(neg_temp[:], row_consts["temp"][:], -1.0, None, ALU.mult)
+
+        v_scale = keep.tile([P, S], U8, name="v_scale", align_bytes=64)
+        nc.vector.tensor_copy(out=v_scale[:], in_=tab_scale[:].indirect(idx_list[:]))
+        v_code = [keep.tile([P, S], U32, name=f"v_code{a}", align_bytes=64) for a in range(KP)]
+
+        def round_w1(raw, dealt, cols, on_scalar):
+            q0, q1 = cols.start // PACK, cols.stop // PACK
+            dst = dealt[:].rearrange("p (t q j) -> p q j t", t=PACK, j=PACK)[:, q0:q1]
+            src = raw[:, :, cols].rearrange("p j (q t) -> p q j t", t=PACK)
+            if on_scalar:
+                nc.scalar.copy(out=dst, in_=src)
+            else:
+                nc.vector.tensor_copy(out=dst, in_=src)
+
+        def first_pass(b, a, raw, shares, banks):
+            dealt = stage.tile([P, PACK * GROUP], BF16, name="w1_dealt", align_bytes=64)
+            code = keep.tile([P, GROUP], U32, name=f"w1_code{b}{a}", tag=f"w1_code{b}{a}", align_bytes=64)
+            scale = keep.tile([P, GROUP], U8, name=f"w1_scale{b}{a}", align_bytes=64)
+            for cols, on_scalar in shares:
+                round_w1(raw, dealt, cols, on_scalar)
+            calls = PACK if a == KP - 1 else 1
+            words = GROUP // calls
+            for c in range(calls):
+                nc.vector.quantize_mx(
+                    out=code[:, c * words : (c + 1) * words].bitcast(FP8X4),
+                    scales=scale[:, c * words : (c + 1) * words],
+                    in_=dealt[:, PACK * c * words : PACK * (c + 1) * words],
+                )
+            for t in range(PACK):
+                for hf in range(S // BANK):
+                    cols = slice(hf * BANK, (hf + 1) * BANK)
+                    nc.tensor.matmul_mx(
+                        out=banks[t, hf][:],
+                        lhsT=code[:, t * P : (t + 1) * P].bitcast(FP8X4),
+                        lhsT_scale=scale[:, t * P : (t + 1) * P],
+                        rhs=v_code[a][:, cols].bitcast(FP8X4),
+                        rhs_scale=v_scale[4 * a : P, cols],
+                        start=(a == 0),
+                        stop=(a == KP - 1),
+                    )
+
+        def h_banks():
+            return {
+                (t, hf): psum.tile([P, BANK], F32, name=f"bank{t}{hf}", tag=f"bank{t}{hf}")
+                for t in range(PACK) for hf in range(S // BANK)
+            }
+
+        def empty_h(b, t, banks, tops):
+            h = keep.tile([P, S], F32, name=f"h{b}{t}")
+            for hf in range(S // BANK):
+                nc.vector.tensor_scalar(
+                    h[:, hf * BANK : (hf + 1) * BANK], banks[t, hf][:], 1.0, None, ALU.mult, ALU.max,
+                    accum_out=tops[:, hf, t : t + 1],
+                )
+            return h
+
+        whole = slice(0, GROUP)
+        left, right = slice(0, GROUP // 2), slice(GROUP // 2, GROUP)
+
+        banks = h_banks()
+        for a in range(KP):
+            nc.vector.tensor_copy(out=v_code[a][:], in_=tab[a][:].indirect(idx_list[:]))
+            shares = [(left, True), (right, False)] if a == KP - 1 else [(whole, True)]
+            first_pass(0, a, w1_raw[0, a], shares, banks)
+
+        for a in range(KP):
+            w1_raw[1, a] = load_w1(1, a, 1)
+        mix_t = []
+        for b in range(RB):
+            mt = ring.tile([P, PACK, M], F32, name=f"mix{b}", tag="rows")
+            nc.sync.dma_start(out=mt[:], in_=mix[b * GROUP : (b + 1) * GROUP, :].rearrange("(p t) m -> p t m", t=PACK))
+            mix_t.append(mt)
+        tenor_t = ring.tile([P, PACK, M], F32, name="tenor_t", tag="rows")
+        nc.sync.dma_start(out=tenor_t[:], in_=tenor.rearrange("(p t) m -> p t m", t=PACK))
+
+        def look_exp(b, t, h, bias, out, offsets):
+            col = b * PACK + t
+            nc.scalar.activation(
+                out=out, in_=h[:].indirect(offsets), func=ACT.Exp,
+                bias=bias[:, t : t + 1], scale=row_consts["temp"][:, col : col + 1],
+            )
+
+        def look_gate(b, t, h, out):
+            col = b * PACK + t
+            nc.scalar.activation(
+                out=out, in_=h[:].indirect(p2_list[:]), func=ACT.Sigmoid,
+                bias=row_consts["thr"][:, col : col + 1], scale=row_consts["steep"][:, col : col + 1],
+            )
+
+        tops0 = keep.tile([P, 2, PACK], F32, name="tops0")
+        bias0 = keep.tile([P, PACK], F32, name="bias0", tag="gate0")
+        a0 = keep.tile([P, PACK, M], F32, name="a0", tag="big0", align_bytes=64)
+        h0 = []
+        for t in range(PACK):
+            h0.append(empty_h(0, t, banks, tops0))
+            nc.vector.tensor_scalar(
+                bias0[:, t : t + 1], tops0[:, 0, t : t + 1], tops0[:, 1, t : t + 1], neg_temp[:, t : t + 1],
+                ALU.max, ALU.mult,
+            )
+            look_exp(0, t, h0[t], bias0, a0[:, t, :], p1_list[:])
+
+        banks = h_banks()
+        for a in range(KP):
+            shares = [(whole, a == 0)]
+            first_pass(1, a, w1_raw[1, a], shares, banks)
+
+        c0 = keep.tile([P, PACK, M], F32, name="c0", tag="gate0")
+        for t in range(PACK):
+            look_gate(0, t, h0[t], c0[:, t, :])
+
+        tops1 = keep.tile([P, 2, PACK], F32, name="tops1")
+        c1 = keep.tile([P, PACK, M], F32, name="c1", tag="big2", align_bytes=64)
+        h1 = []
+        for t in range(PACK):
+            h1.append(empty_h(1, t, banks, tops1))
+            look_gate(1, t, h1[t], c1[:, t, :])
+        top1 = keep.tile([P, PACK], F32, name="top1")
+        bias1 = keep.tile([P, PACK], F32, name="bias1")
+        nc.vector.tensor_tensor(top1[:], tops1[:, 0, :], tops1[:, 1, :], ALU.max)
+        nc.vector.tensor_tensor(bias1[:], top1[:], neg_temp[:, PACK : 2 * PACK], ALU.mult)
+        a1 = keep.tile([P, 2, PACK, HALF], F32, name="a1", tag="big1", align_bytes=64)
+        for hf in range(2):
+            for t in range(PACK):
+                look_exp(1, t, h1[t], bias1, a1[:, hf, t, :], p1_list[:, hf * HALF // 16 : (hf + 1) * HALF // 16])
+
+        def factor(b, c):
+            fac = keep.tile([P, PACK, M], F32, name=f"fac{b}", tag=f"w1_code{1 - b}{KP - 1}", align_bytes=64)
+            nc.vector.tensor_tensor(fac[:], c[:], mix_t[b][:], ALU.mult)
+            for t in range(PACK):
+                col = b * PACK + t
+                nc.vector.tensor_scalar(
+                    fac[:, t, :], fac[:, t, :], row_consts["tilt"][:, col : col + 1], None, ALU.add
+                )
+            return fac
+
+        def woven(flat):
+            return flat.rearrange("p (c i t) -> p c t i", i=4, t=PACK)
+
+        def by_lines(planes):
+            return planes.rearrange("p t (c i) -> p c t i", i=4)
+
+        def make_z(name, fac, a_vals, width):
+            z_bf = keep.tile([P, PACK * width], BF16, name=f"z_bf{name}", align_bytes=64)
+            code = keep.tile([P, width], U32, name=f"z_code{name}", align_bytes=64)
+            scale = keep.tile([P, width], U8, name=f"z_scale{name}", align_bytes=64)
+            nc.vector.tensor_tensor(woven(z_bf[:]), by_lines(fac), by_lines(a_vals), ALU.mult)
+            nc.vector.quantize_mx(out=code[:].bitcast(FP8X4), scales=scale[:], in_=z_bf[:])
+            return code, scale
+
+        y_banks = [psum.tile([P, PACK, QUARTER], F32, name=f"ybank{qd}", tag=f"bank{qd}0") for qd in range(4)]
+
+        def second_pass(b, qd, code, scale):
+            for t in range(PACK):
+                nc.tensor.matmul_mx(
+                    out=y_banks[qd][:, t, :],
+                    lhsT=w4_code[:, b, 2 * P * t : 2 * P * (t + 1)].bitcast(FP4X4),
+                    lhsT_scale=w4_scale[:, b, P * t : P * (t + 1)],
+                    rhs=code.bitcast(FP8X4),
+                    rhs_scale=scale,
+                    start=(b == 0 and t == 0),
+                    stop=(b == RB - 1 and t == PACK - 1),
+                )
+
+        def quarter(qd):
+            return slice(qd * QUARTER, (qd + 1) * QUARTER)
+
+        fac0 = factor(0, c0)
+        z_code, z_scale = make_z("0", fac0[:], a0[:], M)
+        for qd in range(4):
+            second_pass(0, qd, z_code[:, quarter(qd)], z_scale[:, quarter(qd)])
+        fac1 = factor(1, c1)
+        z_code, z_scale = make_z("1a", fac1[:, :, 0:HALF], a1[:, 0], HALF)
+        for qd in range(2):
+            second_pass(1, qd, z_code[:, quarter(qd)], z_scale[:, quarter(qd)])
+        for qd in range(2, 4):
+            z_code, z_scale = make_z(f"1{qd}", fac1[:, :, quarter(qd)], a1[:, 1, :, quarter(qd - 2)], QUARTER)
+            second_pass(1, qd, z_code[:], z_scale[:])
+
+        y_scale = keep.tile([P, M], U8, name="y_scale", align_bytes=64)
+        out_rows = out_0.rearrange("(p t) m -> p t m", t=PACK)
+        out_words = out_1[0].rearrange("p m t -> p (m t)")
+        for hf in range(2):
+            cols = slice(hf * HALF, (hf + 1) * HALF)
+            y = keep.tile([P, PACK, HALF], F32, name=f"y{hf}")
+            y_bf = keep.tile([P, PACK * HALF], BF16, name=f"y_bf{hf}", align_bytes=64)
+            y_code = keep.tile([P, HALF], U32, name=f"y_code{hf}", align_bytes=64)
+            for s in range(2):
+                qd = 2 * hf + s
+                nc.vector.tensor_tensor(y[:, :, quarter(s)], y_banks[qd][:], tenor_t[:, :, quarter(qd)], ALU.mult)
+                dst = woven(y_bf[:, PACK * QUARTER * s : PACK * QUARTER * (s + 1)])
+                if qd < 3:
+                    nc.scalar.copy(out=dst, in_=by_lines(y[:, :, quarter(s)]))
+                else:
+                    nc.vector.tensor_copy(out=dst, in_=by_lines(y[:, :, quarter(s)]))
+            nc.sync.dma_start(out=out_rows[:, :, cols], in_=y[:])
+            nc.vector.quantize_mx(out=y_code[:].bitcast(FP8X4), scales=y_scale[:, cols], in_=y_bf[:])
+            nc.sync.dma_start(
+                out=out_words[:, PACK * hf * HALF : PACK * (hf + 1) * HALF].bitcast(I32), in_=y_code[:].bitcast(I32)
+            )
+        for quad in range(4):
+            queue = nc.scalar if quad % 2 == 0 else nc.sync
+            queue.dma_start(
+                out=out_2[0, 4 * quad : 4 * quad + 4, :].bitcast(I32),
+                in_=y_scale[32 * quad : 32 * quad + 4, :].bitcast(I32),
+            )

@@ -62,6 +62,12 @@ def tile_list_swap_tenor_pressure_kernel(
                 nc.sync.dma_start(out=raw[:, :, cols], in_=rows[:, :, cols])
             return raw
 
+        scale_rows = keep.tile([P, T // 4], I32, name="scale_rows")
+        for quad in range(4):
+            nc.gpsimd.dma_start(
+                out=scale_rows[32 * quad : 32 * quad + 4 * KP, :],
+                in_=tab_scales[:, 4 * quad : 4 * quad + 4, :].bitcast(I32),
+            )
         row_consts = {}
         for name, vec in (("temp", temp), ("steep", steep), ("thr", thr), ("tilt", tilt)):
             tile_v = keep.tile([P, RB * PACK], F32, name=f"{name}_cols")
@@ -72,12 +78,8 @@ def tile_list_swap_tenor_pressure_kernel(
             row_consts[name] = tile_v
         nc.sync.dma_start(idx_list[:], offs)
         load_tab(0)
-        scale_rows = keep.tile([P, T // 4], I32, name="scale_rows")
-        for quad in range(4):
-            nc.sync.dma_start(
-                out=scale_rows[32 * quad : 32 * quad + 4 * KP, :],
-                in_=tab_scales[:, 4 * quad : 4 * quad + 4, :].bitcast(I32),
-            )
+        nc.sync.dma_start(p1_list[:], pos1)
+        nc.sync.dma_start(p2_list[:], pos2)
         w1_raw = {}
         w1_raw[0, 0] = load_w1(0, 0, 1)
         load_tab(1)
@@ -90,8 +92,6 @@ def tile_list_swap_tenor_pressure_kernel(
             )
         load_tab(2)
         w1_raw[0, 2] = load_w1(0, 2, 2)
-        nc.sync.dma_start(p1_list[:], pos1)
-        nc.sync.dma_start(p2_list[:], pos2)
 
         for quad in range(4):
             rows = slice(32 * quad, 32 * quad + 4 * KP)
@@ -237,7 +237,11 @@ def tile_list_swap_tenor_pressure_kernel(
 
         def factor(b, c):
             fac = keep.tile([P, PACK, M], F32, name=f"fac{b}", tag=f"w1_code{1 - b}{KP - 1}", align_bytes=64)
-            nc.vector.tensor_tensor(fac[:], c[:], mix_t[b][:], ALU.mult)
+            if b == 0:
+                for t in range(PACK):
+                    nc.gpsimd.tensor_tensor(fac[:, t, :], c[:, t, :], mix_t[b][:, t, :], ALU.mult)
+            else:
+                nc.vector.tensor_tensor(fac[:], c[:], mix_t[b][:], ALU.mult)
             for t in range(PACK):
                 col = b * PACK + t
                 nc.vector.tensor_scalar(

@@ -34,7 +34,6 @@ def tile_list_swap_tenor_pressure_kernel(
     with ExitStack() as ctx:
         lists = ctx.enter_context(tc.tile_pool(name="lists", bufs=1))
         keep = ctx.enter_context(tc.tile_pool(name="keep", bufs=1))
-        stage = ctx.enter_context(tc.tile_pool(name="stage", bufs=3))
         ring = ctx.enter_context(tc.tile_pool(name="ring", bufs=RB * KP))
         psum = ctx.enter_context(tc.psum_pool(name="psum", bufs=1))
 
@@ -124,32 +123,34 @@ def tile_list_swap_tenor_pressure_kernel(
             else:
                 nc.vector.tensor_copy(out=dst, in_=src)
 
-        def first_pass(b, a, raw, shares, banks):
-            dealt = stage.tile([P, PACK * GROUP], BF16, name="w1_dealt", align_bytes=64)
+        def w1_tiles(b, a):
+            dealt = keep.tile([P, PACK * GROUP], BF16, name=f"w1_dealt{b}{a}", tag=f"dealt{a}", align_bytes=64)
             code = keep.tile([P, GROUP], U32, name=f"w1_code{b}{a}", tag=f"w1_code{b}{a}", align_bytes=64)
             scale = keep.tile([P, GROUP], U8, name=f"w1_scale{b}{a}", align_bytes=64)
-            for cols, on_scalar in shares:
-                round_w1(raw, dealt, cols, on_scalar)
-            calls = PACK if a == KP - 1 else 1
-            words = GROUP // calls
-            for c in range(calls):
-                nc.vector.quantize_mx(
-                    out=code[:, c * words : (c + 1) * words].bitcast(FP8X4),
-                    scales=scale[:, c * words : (c + 1) * words],
-                    in_=dealt[:, PACK * c * words : PACK * (c + 1) * words],
+            return dealt, code, scale
+
+        def quantise_w1(tiles, first_t, last_t):
+            dealt, code, scale = tiles
+            words = slice(first_t * P, (last_t + 1) * P)
+            nc.vector.quantize_mx(
+                out=code[:, words].bitcast(FP8X4),
+                scales=scale[:, words],
+                in_=dealt[:, PACK * words.start : PACK * words.stop],
+            )
+
+        def first_pass(a, t, tiles, banks):
+            dealt, code, scale = tiles
+            for hf in range(S // BANK):
+                cols = slice(hf * BANK, (hf + 1) * BANK)
+                nc.tensor.matmul_mx(
+                    out=banks[t, hf][:],
+                    lhsT=code[:, t * P : (t + 1) * P].bitcast(FP8X4),
+                    lhsT_scale=scale[:, t * P : (t + 1) * P],
+                    rhs=v_code[a][:, cols].bitcast(FP8X4),
+                    rhs_scale=v_scale[4 * a : P, cols],
+                    start=(a == 0),
+                    stop=(a == KP - 1),
                 )
-            for t in range(PACK):
-                for hf in range(S // BANK):
-                    cols = slice(hf * BANK, (hf + 1) * BANK)
-                    nc.tensor.matmul_mx(
-                        out=banks[t, hf][:],
-                        lhsT=code[:, t * P : (t + 1) * P].bitcast(FP8X4),
-                        lhsT_scale=scale[:, t * P : (t + 1) * P],
-                        rhs=v_code[a][:, cols].bitcast(FP8X4),
-                        rhs_scale=v_scale[4 * a : P, cols],
-                        start=(a == 0),
-                        stop=(a == KP - 1),
-                    )
 
         def h_banks():
             return {
@@ -157,14 +158,11 @@ def tile_list_swap_tenor_pressure_kernel(
                 for t in range(PACK) for hf in range(S // BANK)
             }
 
-        def empty_h(b, t, banks, tops):
-            h = keep.tile([P, S], F32, name=f"h{b}{t}")
-            for hf in range(S // BANK):
-                nc.vector.tensor_scalar(
-                    h[:, hf * BANK : (hf + 1) * BANK], banks[t, hf][:], 1.0, None, ALU.mult, ALU.max,
-                    accum_out=tops[:, hf, t : t + 1],
-                )
-            return h
+        def empty_bank(b, t, hf, banks):
+            nc.vector.tensor_scalar(
+                h[b, t][:, hf * BANK : (hf + 1) * BANK], banks[t, hf][:], 1.0, None, ALU.mult, ALU.max,
+                accum_out=tops[:, hf, b * PACK + t : b * PACK + t + 1],
+            )
 
         whole = slice(0, GROUP)
         left, right = slice(0, GROUP // 2), slice(GROUP // 2, GROUP)
@@ -172,8 +170,17 @@ def tile_list_swap_tenor_pressure_kernel(
         banks = h_banks()
         for a in range(KP):
             nc.vector.tensor_copy(out=v_code[a][:], in_=tab[a][:].indirect(idx_list[:]))
-            shares = [(left, True), (right, False)] if a == KP - 1 else [(whole, True)]
-            first_pass(0, a, w1_raw[0, a], shares, banks)
+            tiles = w1_tiles(0, a)
+            if a < KP - 1:
+                round_w1(w1_raw[0, a], tiles[0], whole, True)
+                quantise_w1(tiles, 0, PACK - 1)
+            else:
+                round_w1(w1_raw[0, a], tiles[0], left, True)
+                round_w1(w1_raw[0, a], tiles[0], right, False)
+                for t in range(PACK):
+                    quantise_w1(tiles, t, t)
+            for t in range(PACK):
+                first_pass(a, t, tiles, banks)
 
         for a in range(KP):
             w1_raw[1, a] = load_w1(1, a, 1)
@@ -182,8 +189,6 @@ def tile_list_swap_tenor_pressure_kernel(
             mt = ring.tile([P, PACK, M], F32, name=f"mix{b}", tag="rows")
             nc.sync.dma_start(out=mt[:], in_=mix[b * GROUP : (b + 1) * GROUP, :].rearrange("(p t) m -> p t m", t=PACK))
             mix_t.append(mt)
-        tenor_t = ring.tile([P, PACK, M], F32, name="tenor_t", tag="rows")
-        nc.sync.dma_start(out=tenor_t[:], in_=tenor.rearrange("(p t) m -> p t m", t=PACK))
 
         def look_exp(b, t, h, bias, out, offsets):
             col = b * PACK + t
@@ -199,49 +204,73 @@ def tile_list_swap_tenor_pressure_kernel(
                 bias=row_consts["thr"][:, col : col + 1], scale=row_consts["steep"][:, col : col + 1],
             )
 
-        tops0 = keep.tile([P, 2, PACK], F32, name="tops0")
+        tops = keep.tile([P, 2, RB * PACK], F32, name="tops")
+        h = {(b, t): keep.tile([P, S], F32, name=f"h{b}{t}") for b in range(RB) for t in range(PACK)}
+        later = [w1_tiles(1, a) for a in range(KP)]
         bias0 = keep.tile([P, PACK], F32, name="bias0", tag="gate0")
         a0 = keep.tile([P, PACK, M], F32, name="a0", tag="big0", align_bytes=64)
-        h0 = []
-        for t in range(PACK):
-            h0.append(empty_h(0, t, banks, tops0))
+
+        def first_look(t):
             nc.vector.tensor_scalar(
-                bias0[:, t : t + 1], tops0[:, 0, t : t + 1], tops0[:, 1, t : t + 1], neg_temp[:, t : t + 1],
+                bias0[:, t : t + 1], tops[:, 0, t : t + 1], tops[:, 1, t : t + 1], neg_temp[:, t : t + 1],
                 ALU.max, ALU.mult,
             )
-            look_exp(0, t, h0[t], bias0, a0[:, t, :], p1_list[:])
+            look_exp(0, t, h[0, t], bias0, a0[:, t, :], p1_list[:])
+
+        round_w1(w1_raw[1, 0], later[0][0], whole, True)
+        for t in range(PACK):
+            empty_bank(0, t, 0, banks)
+            if t > 0:
+                first_look(t - 1)
+            empty_bank(0, t, 1, banks)
+            if t == PACK - 2:
+                quantise_w1(later[0], 0, PACK - 1)
+        first_look(PACK - 1)
 
         banks = h_banks()
-        for a in range(KP):
-            shares = [(whole, a == 0)]
-            first_pass(1, a, w1_raw[1, a], shares, banks)
+        for t in range(PACK):
+            first_pass(0, t, later[0], banks)
+        for a in range(1, KP):
+            round_w1(w1_raw[1, a], later[a][0], whole, False)
+        for t in range(PACK):
+            for a in range(1, KP):
+                quantise_w1(later[a], t, t)
+        for t in range(PACK):
+            for a in range(1, KP):
+                first_pass(a, t, later[a], banks)
+
+        tenor_rows = tenor.rearrange("(p t) m -> p t m", t=PACK)
+        tenor_t = []
+        for hf in range(2):
+            tt = keep.tile([P, PACK, HALF], F32, name=f"tenor{hf}", tag=f"dealt{hf}", align_bytes=64)
+            nc.sync.dma_start(out=tt[:], in_=tenor_rows[:, :, hf * HALF : (hf + 1) * HALF])
+            tenor_t.append(tt)
 
         c0 = keep.tile([P, PACK, M], F32, name="c0", tag="gate0")
         for t in range(PACK):
-            look_gate(0, t, h0[t], c0[:, t, :])
-
-        tops1 = keep.tile([P, 2, PACK], F32, name="tops1")
+            look_gate(0, t, h[0, t], c0[:, t, :])
         c1 = keep.tile([P, PACK, M], F32, name="c1", tag="big2", align_bytes=64)
-        h1 = []
         for t in range(PACK):
-            h1.append(empty_h(1, t, banks, tops1))
-            look_gate(1, t, h1[t], c1[:, t, :])
+            for hf in range(S // BANK):
+                empty_bank(1, t, hf, banks)
+            look_gate(1, t, h[1, t], c1[:, t, :])
         top1 = keep.tile([P, PACK], F32, name="top1")
         bias1 = keep.tile([P, PACK], F32, name="bias1")
-        nc.vector.tensor_tensor(top1[:], tops1[:, 0, :], tops1[:, 1, :], ALU.max)
+        nc.vector.tensor_tensor(top1[:], tops[:, 0, PACK : 2 * PACK], tops[:, 1, PACK : 2 * PACK], ALU.max)
         nc.vector.tensor_tensor(bias1[:], top1[:], neg_temp[:, PACK : 2 * PACK], ALU.mult)
         a1 = keep.tile([P, 2, PACK, HALF], F32, name="a1", tag="big1", align_bytes=64)
         for hf in range(2):
             for t in range(PACK):
-                look_exp(1, t, h1[t], bias1, a1[:, hf, t, :], p1_list[:, hf * HALF // 16 : (hf + 1) * HALF // 16])
+                look_exp(1, t, h[1, t], bias1, a1[:, hf, t, :], p1_list[:, hf * HALF // 16 : (hf + 1) * HALF // 16])
 
         def factor(b, c):
-            fac = keep.tile([P, PACK, M], F32, name=f"fac{b}", tag=f"w1_code{1 - b}{KP - 1}", align_bytes=64)
+            fac = keep.tile([P, PACK, M], F32, name=f"fac{b}", tag=("dealt2" if b == 0 else "w1_code02"), align_bytes=64)
             if b == 0:
                 for t in range(PACK):
                     nc.gpsimd.tensor_tensor(fac[:, t, :], c[:, t, :], mix_t[b][:, t, :], ALU.mult)
             else:
-                nc.vector.tensor_tensor(fac[:], c[:], mix_t[b][:], ALU.mult)
+                for t in range(0, PACK, 2):
+                    nc.vector.tensor_tensor(fac[:, t : t + 2, :], c[:, t : t + 2, :], mix_t[b][:, t : t + 2, :], ALU.mult)
             for t in range(PACK):
                 col = b * PACK + t
                 nc.vector.tensor_scalar(
@@ -255,12 +284,15 @@ def tile_list_swap_tenor_pressure_kernel(
         def by_lines(planes):
             return planes.rearrange("p t (c i) -> p c t i", i=4)
 
-        def make_z(name, fac, a_vals, width):
-            z_bf = keep.tile([P, PACK * width], BF16, name=f"z_bf{name}", align_bytes=64)
+        def round_z(name, fac, a_part, width, tag):
+            z_bf = keep.tile([P, PACK * width], BF16, name=f"z_bf{name}", tag=tag, align_bytes=64)
+            nc.vector.tensor_tensor(woven(z_bf[:]), by_lines(fac), by_lines(a_part), ALU.mult)
+            return z_bf
+
+        def quantise_z(name, z_bf, width):
             code = keep.tile([P, width], U32, name=f"z_code{name}", align_bytes=64)
             scale = keep.tile([P, width], U8, name=f"z_scale{name}", align_bytes=64)
-            nc.vector.tensor_tensor(woven(z_bf[:]), by_lines(fac), by_lines(a_vals), ALU.mult)
-            nc.vector.quantize_mx(out=code[:].bitcast(FP8X4), scales=scale[:], in_=z_bf[:])
+            nc.vector.quantize_mx(out=code[:].bitcast(FP8X4), scales=scale[:], in_=z_bf)
             return code, scale
 
         y_banks = [psum.tile([P, PACK, QUARTER], F32, name=f"ybank{qd}", tag=f"bank{qd}0") for qd in range(4)]
@@ -280,39 +312,60 @@ def tile_list_swap_tenor_pressure_kernel(
         def quarter(qd):
             return slice(qd * QUARTER, (qd + 1) * QUARTER)
 
+        def half(hf):
+            return slice(hf * HALF, (hf + 1) * HALF)
+
+        def multiply_half(b, hf, z_bf):
+            z_code, z_scale = quantise_z(f"{b}{hf}", z_bf[:], HALF)
+            for s in range(2):
+                second_pass(b, 2 * hf + s, z_code[:, quarter(s)], z_scale[:, quarter(s)])
+
         fac0 = factor(0, c0)
-        z_code, z_scale = make_z("0", fac0[:], a0[:], M)
-        for qd in range(4):
-            second_pass(0, qd, z_code[:, quarter(qd)], z_scale[:, quarter(qd)])
+        z0 = [round_z(f"0{hf}", fac0[:, :, half(hf)], a0[:, :, half(hf)], HALF, f"z_bf0{hf}") for hf in range(2)]
+        for hf in range(2):
+            multiply_half(0, hf, z0[hf])
         fac1 = factor(1, c1)
-        z_code, z_scale = make_z("1a", fac1[:, :, 0:HALF], a1[:, 0], HALF)
-        for qd in range(2):
-            second_pass(1, qd, z_code[:, quarter(qd)], z_scale[:, quarter(qd)])
-        for qd in range(2, 4):
-            z_code, z_scale = make_z(f"1{qd}", fac1[:, :, quarter(qd)], a1[:, 1, :, quarter(qd - 2)], QUARTER)
-            second_pass(1, qd, z_code[:], z_scale[:])
+        multiply_half(1, 0, round_z("10", fac1[:, :, half(0)], a1[:, 0], HALF, "z_bf10"))
 
         y_scale = keep.tile([P, M], U8, name="y_scale", align_bytes=64)
         out_rows = out_0.rearrange("(p t) m -> p t m", t=PACK)
         out_words = out_1[0].rearrange("p m t -> p (m t)")
-        for hf in range(2):
+
+        def finish(hf):
             cols = slice(hf * HALF, (hf + 1) * HALF)
             y = keep.tile([P, PACK, HALF], F32, name=f"y{hf}")
             y_bf = keep.tile([P, PACK * HALF], BF16, name=f"y_bf{hf}", align_bytes=64)
-            y_code = keep.tile([P, HALF], U32, name=f"y_code{hf}", align_bytes=64)
             for s in range(2):
                 qd = 2 * hf + s
-                nc.vector.tensor_tensor(y[:, :, quarter(s)], y_banks[qd][:], tenor_t[:, :, quarter(qd)], ALU.mult)
+                nc.vector.tensor_tensor(y[:, :, quarter(s)], y_banks[qd][:], tenor_t[hf][:, :, quarter(s)], ALU.mult)
                 dst = woven(y_bf[:, PACK * QUARTER * s : PACK * QUARTER * (s + 1)])
                 if qd < 3:
                     nc.scalar.copy(out=dst, in_=by_lines(y[:, :, quarter(s)]))
                 else:
                     nc.vector.tensor_copy(out=dst, in_=by_lines(y[:, :, quarter(s)]))
             nc.sync.dma_start(out=out_rows[:, :, cols], in_=y[:])
+            return y_bf
+
+        def planes(hf, y_bf):
+            cols = slice(hf * HALF, (hf + 1) * HALF)
+            y_code = keep.tile([P, HALF], U32, name=f"y_code{hf}", align_bytes=64)
             nc.vector.quantize_mx(out=y_code[:].bitcast(FP8X4), scales=y_scale[:, cols], in_=y_bf[:])
             nc.sync.dma_start(
                 out=out_words[:, PACK * hf * HALF : PACK * (hf + 1) * HALF].bitcast(I32), in_=y_code[:].bitcast(I32)
             )
+
+        y_bf0 = finish(0)
+        last = keep.tile([P, PACK * HALF], BF16, name="z_bf_last", tag="dealt0", align_bytes=64)
+        for s in range(2):
+            nc.vector.tensor_tensor(
+                woven(last[:, PACK * QUARTER * s : PACK * QUARTER * (s + 1)]),
+                by_lines(fac1[:, :, quarter(2 + s)]), by_lines(a1[:, 1, :, quarter(s)]), ALU.mult,
+            )
+        for s in range(2):
+            z_code, z_scale = quantise_z(f"q{s}", last[:, PACK * QUARTER * s : PACK * QUARTER * (s + 1)], QUARTER)
+            second_pass(1, 2 + s, z_code[:], z_scale[:])
+        planes(0, y_bf0)
+        planes(1, finish(1))
         for quad in range(4):
             queue = nc.scalar if quad % 2 == 0 else nc.sync
             queue.dma_start(

@@ -116,12 +116,13 @@ def tile_list_swap_tenor_pressure_kernel(
 
         def round_w1(raw, dealt, cols, on_scalar):
             q0, q1 = cols.start // PACK, cols.stop // PACK
-            dst = dealt[:].rearrange("p (t q j) -> p q j t", t=PACK, j=PACK)[:, q0:q1]
-            src = raw[:, :, cols].rearrange("p j (q t) -> p q j t", t=PACK)
-            if on_scalar:
-                nc.scalar.copy(out=dst, in_=src)
-            else:
-                nc.vector.tensor_copy(out=dst, in_=src)
+            for t0 in range(0, PACK, 2):
+                dst = dealt[:].rearrange("p (t q j) -> p q j t", t=PACK, j=PACK)[:, q0:q1, :, t0 : t0 + 2]
+                src = raw[:, :, cols].rearrange("p j (q t) -> p q j t", t=PACK)[:, :, :, t0 : t0 + 2]
+                if on_scalar:
+                    nc.scalar.copy(out=dst, in_=src)
+                else:
+                    nc.vector.tensor_copy(out=dst, in_=src)
 
         def w1_tiles(b, a):
             dealt = keep.tile([P, PACK * GROUP], BF16, name=f"w1_dealt{b}{a}", tag=f"dealt{a}", align_bytes=64)

@@ -61,54 +61,39 @@ def tile_list_swap_tenor_pressure_kernel(
                 nc.sync.dma_start(out=raw[:, :, cols], in_=rows[:, :, cols])
             return raw
 
-        scale_rows = keep.tile([P, T // 4], I32, name="scale_rows")
         for quad in range(4):
             nc.gpsimd.dma_start(
-                out=scale_rows[32 * quad : 32 * quad + 4 * KP, :],
+                out=tab_scale[32 * quad : 32 * quad + 4 * KP, :].bitcast(I32),
                 in_=tab_scales[:, 4 * quad : 4 * quad + 4, :].bitcast(I32),
             )
+        nc.sync.dma_start(idx_list[:], offs)
+        nc.sync.dma_start(p1_list[:], pos1)
+        nc.sync.dma_start(p2_list[:], pos2)
+        load_tab(0)
+        w1_raw = {}
+        w1_raw[0, 0] = load_w1(0, 0, 1)
+        w1_raw[0, 1] = load_w1(0, 1, 1)
         row_consts = {}
         for name, vec in (("temp", temp), ("steep", steep), ("thr", thr), ("tilt", tilt)):
             tile_v = keep.tile([P, RB * PACK], F32, name=f"{name}_cols")
-            nc.gpsimd.dma_start(
+            nc.sync.dma_start(
                 out=tile_v[:].rearrange("p (b t) -> p b t", t=PACK),
                 in_=vec.rearrange("(b p t) -> p b t", b=RB, t=PACK),
             )
             row_consts[name] = tile_v
-        nc.sync.dma_start(idx_list[:], offs)
-        load_tab(0)
-        nc.sync.dma_start(p1_list[:], pos1)
-        nc.sync.dma_start(p2_list[:], pos2)
-        w1_raw = {}
-        w1_raw[0, 0] = load_w1(0, 0, 1)
-        load_tab(1)
         nc.sync.dma_start(out=w4_raw[:].bitcast(I32), in_=w4_words.rearrange("b p c -> p b c").bitcast(I32))
-        w1_raw[0, 1] = load_w1(0, 1, 1)
-        for quad in range(4):
+
+        def load_w4_scales(quad):
             nc.sync.dma_start(
                 out=w4_scale_raw[32 * quad : 32 * quad + 4].bitcast(I32),
                 in_=w4_scales[:, 4 * quad : 4 * quad + 4, :].rearrange("b r c -> r b c").bitcast(I32),
             )
+
+        load_tab(1)
+        for quad in range(4):
+            load_w4_scales(quad)
         load_tab(2)
         w1_raw[0, 2] = load_w1(0, 2, 2)
-
-        for quad in range(4):
-            rows = slice(32 * quad, 32 * quad + 4 * KP)
-            nc.vector.tensor_copy(out=tab_scale[rows, :].bitcast(I32), in_=scale_rows[rows, :])
-
-        w4_code = keep.tile([P, RB, 2 * N], U8, name="w4_code", align_bytes=64)
-        w4_scale = keep.tile([P, RB, N], U8, name="w4_scale", align_bytes=64)
-        for b in range(RB):
-            nc.vector.tensor_copy(
-                out=w4_code[:, b, :].rearrange("p (t q e) -> p t q e", t=PACK, e=2),
-                in_=w4_raw[:, b, :].rearrange("p (q t e) -> p t q e", t=PACK, e=2),
-            )
-        nc.vector.tensor_copy(
-            out=w4_scale[:].rearrange("p b (t q) -> p b t q", t=PACK),
-            in_=w4_scale_raw[:].rearrange("p b (q t) -> p b t q", t=PACK),
-        )
-        neg_temp = keep.tile([P, RB * PACK], F32, name="neg_temp")
-        nc.vector.tensor_scalar(neg_temp[:], row_consts["temp"][:], -1.0, None, ALU.mult)
 
         v_scale = keep.tile([P, S], U8, name="v_scale", align_bytes=64)
         nc.vector.tensor_copy(out=v_scale[:], in_=tab_scale[:].indirect(idx_list[:]))
@@ -183,6 +168,18 @@ def tile_list_swap_tenor_pressure_kernel(
             for t in range(PACK):
                 first_pass(a, t, tiles, banks)
 
+        w4_code = keep.tile([P, RB, 2 * N], U8, name="w4_code", tag="big0", align_bytes=64)
+        w4_scale = keep.tile([P, RB, N], U8, name="w4_scale", tag="big1", align_bytes=64)
+        for b in range(RB):
+            nc.vector.tensor_copy(
+                out=w4_code[:, b, :].rearrange("p (t q e) -> p t q e", t=PACK, e=2),
+                in_=w4_raw[:, b, :].rearrange("p (q t e) -> p t q e", t=PACK, e=2),
+            )
+        nc.vector.tensor_copy(
+            out=w4_scale[:].rearrange("p b (t q) -> p b t q", t=PACK),
+            in_=w4_scale_raw[:].rearrange("p b (q t) -> p b t q", t=PACK),
+        )
+
         for a in range(KP):
             w1_raw[1, a] = load_w1(1, a, 1)
         mix_t = []
@@ -205,11 +202,13 @@ def tile_list_swap_tenor_pressure_kernel(
                 bias=row_consts["thr"][:, col : col + 1], scale=row_consts["steep"][:, col : col + 1],
             )
 
+        neg_temp = keep.tile([P, RB * PACK], F32, name="neg_temp")
+        nc.vector.tensor_scalar(neg_temp[:], row_consts["temp"][:], -1.0, None, ALU.mult)
         tops = keep.tile([P, 2, RB * PACK], F32, name="tops")
         h = {(b, t): keep.tile([P, S], F32, name=f"h{b}{t}") for b in range(RB) for t in range(PACK)}
         later = [w1_tiles(1, a) for a in range(KP)]
         bias0 = keep.tile([P, PACK], F32, name="bias0", tag="gate0")
-        a0 = keep.tile([P, PACK, M], F32, name="a0", tag="big0", align_bytes=64)
+        a0 = ring.tile([P, PACK, M], F32, name="a0", tag="rows")
 
         def first_look(t):
             nc.vector.tensor_scalar(
@@ -259,7 +258,7 @@ def tile_list_swap_tenor_pressure_kernel(
         bias1 = keep.tile([P, PACK], F32, name="bias1")
         nc.vector.tensor_tensor(top1[:], tops[:, 0, PACK : 2 * PACK], tops[:, 1, PACK : 2 * PACK], ALU.max)
         nc.vector.tensor_tensor(bias1[:], top1[:], neg_temp[:, PACK : 2 * PACK], ALU.mult)
-        a1 = keep.tile([P, 2, PACK, HALF], F32, name="a1", tag="big1", align_bytes=64)
+        a1 = ring.tile([P, 2, PACK, HALF], F32, name="a1", tag="rows")
         for hf in range(2):
             for t in range(PACK):
                 look_exp(1, t, h[1, t], bias1, a1[:, hf, t, :], p1_list[:, hf * HALF // 16 : (hf + 1) * HALF // 16])

from contextlib import ExitStack

import concourse.mybir as mybir

K, H, N, T, S, M = 1536, 1024, 512, 4096, 1024, 512
FLOPS = 2 * K * H * S + 2 * H * N * M

F32 = mybir.dt.float32
BF16 = mybir.dt.bfloat16
I32 = mybir.dt.int32
U32 = mybir.dt.uint32
U16 = mybir.dt.uint16
U8 = mybir.dt.uint8
FP8X4 = mybir.dt.float8_e4m3fn_x4
FP4X4 = mybir.dt.float4_e2m1fn_x4
ACT = mybir.ActivationFunctionType
ALU = mybir.AluOpType

P = 128
PACK = 4
GROUP = P * PACK
KP = K // GROUP
RB = H // GROUP
BANK = 512
HALF = M // 2
QUARTER = M // 4


def tile_list_swap_tenor_pressure_kernel(
    tc, tab_words, tab_scales, offs, pos1, pos2, w1, temp, steep, thr, tilt, mix,
    w4_words, w4_scales, tenor, out_0, out_1, out_2,
):
    nc = tc.nc
    with ExitStack() as ctx:
        lists = ctx.enter_context(tc.tile_pool(name="lists", bufs=1))
        keep = ctx.enter_context(tc.tile_pool(name="keep", bufs=1))
        ring = ctx.enter_context(tc.tile_pool(name="ring", bufs=RB * KP))
        psum = ctx.enter_context(tc.psum_pool(name="psum", bufs=1))

        idx_list = lists.tile([P, S // 16], U16, name="idx_list")
        p1_list = lists.tile([P, M // 16], U16, name="p1_list")
        p2_list = lists.tile([P, M // 16], U16, name="p2_list")

        tab_scale = keep.tile([P, T], U8, name="tab_scale", align_bytes=64)
        w4_scale_raw = keep.tile([P, RB, N], U8, name="w4_scale_raw", align_bytes=64)
        w4_raw = keep.tile([P, RB, 2 * N], U8, name="w4_raw", align_bytes=64)
        nc.vector.memset(tab_scale[:].bitcast(I32), 0)
        nc.vector.memset(w4_scale_raw[:].rearrange("p b n -> p (b n)").bitcast(I32), 0)

        tab = [keep.tile([P, T], U32, name=f"tab{a}", tag=f"big{a}", align_bytes=64) for a in range(KP)]

        def load_tab(a):
            nc.sync.dma_start(out=tab[a][:].bitcast(I32), in_=tab_words[a].rearrange("p t i -> p (t i)").bitcast(I32))

        def load_w1(b, a, pieces):
            raw = ring.tile([P, PACK, GROUP], F32, name="w1_raw", tag="rows")
            rows = w1[a * GROUP : (a + 1) * GROUP, b * GROUP : (b + 1) * GROUP].rearrange("(p j) c -> p j c", j=PACK)
            width = GROUP // pieces
            for s in range(pieces):
                cols = slice(s * width, (s + 1) * width)
                nc.sync.dma_start(out=raw[:, :, cols], in_=rows[:, :, cols])
            return raw

        for quad in range(4):
            nc.gpsimd.dma_start(
                out=tab_scale[32 * quad : 32 * quad + 4 * KP, :].bitcast(I32),
                in_=tab_scales[:, 4 * quad : 4 * quad + 4, :].bitcast(I32),
            )
        nc.sync.dma_start(idx_list[:], offs)
        nc.sync.dma_start(p1_list[:], pos1)
        nc.sync.dma_start(p2_list[:], pos2)
        load_tab(0)
        w1_raw = {}
        w1_raw[0, 0] = load_w1(0, 0, 1)
        w1_raw[0, 1] = load_w1(0, 1, 1)
        row_consts = {}
        for name, vec in (("temp", temp), ("steep", steep), ("thr", thr), ("tilt", tilt)):
            tile_v = keep.tile([P, RB * PACK], F32, name=f"{name}_cols")
            nc.sync.dma_start(
                out=tile_v[:].rearrange("p (b t) -> p b t", t=PACK),
                in_=vec.rearrange("(b p t) -> p b t", b=RB, t=PACK),
            )
            row_consts[name] = tile_v
        nc.sync.dma_start(out=w4_raw[:].bitcast(I32), in_=w4_words.rearrange("b p c -> p b c").bitcast(I32))

        def load_w4_scales(quad):
            nc.sync.dma_start(
                out=w4_scale_raw[32 * quad : 32 * quad + 4].bitcast(I32),
                in_=w4_scales[:, 4 * quad : 4 * quad + 4, :].rearrange("b r c -> r b c").bitcast(I32),
            )

        load_tab(1)
        for quad in range(4):
            load_w4_scales(quad)
        load_tab(2)
        w1_raw[0, 2] = load_w1(0, 2, 2)

        v_scale = keep.tile([P, S], U8, name="v_scale", align_bytes=64)
        nc.vector.tensor_copy(out=v_scale[:], in_=tab_scale[:].indirect(idx_list[:]))
        v_code = [keep.tile([P, S], U32, name=f"v_code{a}", align_bytes=64) for a in range(KP)]

        def round_w1(raw, dealt, cols, on_scalar):
            q0, q1 = cols.start // PACK, cols.stop // PACK
            for t0 in range(0, PACK, 2):
                dst = dealt[:].rearrange("p (t q j) -> p q j t", t=PACK, j=PACK)[:, q0:q1, :, t0 : t0 + 2]
                src = raw[:, :, cols].rearrange("p j (q t) -> p q j t", t=PACK)[:, :, :, t0 : t0 + 2]
                if on_scalar:
                    nc.scalar.copy(out=dst, in_=src)
                else:
                    nc.vector.tensor_copy(out=dst, in_=src)

        def w1_tiles(b, a):
            dealt = keep.tile([P, PACK * GROUP], BF16, name=f"w1_dealt{b}{a}", tag=f"dealt{a}", align_bytes=64)
            code = keep.tile([P, GROUP], U32, name=f"w1_code{b}{a}", tag=f"w1_code{b}{a}", align_bytes=64)
            scale = keep.tile([P, GROUP], U8, name=f"w1_scale{b}{a}", align_bytes=64)
            return dealt, code, scale

        def quantise_w1(tiles, first_t, last_t):
            dealt, code, scale = tiles
            words = slice(first_t * P, (last_t + 1) * P)
            nc.vector.quantize_mx(
                out=code[:, words].bitcast(FP8X4),
                scales=scale[:, words],
                in_=dealt[:, PACK * words.start : PACK * words.stop],
            )

        def first_pass(a, t, tiles, banks):
            dealt, code, scale = tiles
            for hf in range(S // BANK):
                cols = slice(hf * BANK, (hf + 1) * BANK)
                nc.tensor.matmul_mx(
                    out=banks[t, hf][:],
                    lhsT=code[:, t * P : (t + 1) * P].bitcast(FP8X4),
                    lhsT_scale=scale[:, t * P : (t + 1) * P],
                    rhs=v_code[a][:, cols].bitcast(FP8X4),
                    rhs_scale=v_scale[4 * a : P, cols],
                    start=(a == 0),
                    stop=(a == KP - 1),
                )

        def h_banks():
            return {
                (t, hf): psum.tile([P, BANK], F32, name=f"bank{t}{hf}", tag=f"bank{t}{hf}")
                for t in range(PACK) for hf in range(S // BANK)
            }

        def empty_bank(b, t, hf, banks):
            nc.vector.tensor_scalar(
                h[b, t][:, hf * BANK : (hf + 1) * BANK], banks[t, hf][:], 1.0, None, ALU.mult, ALU.max,
                accum_out=tops[:, hf, b * PACK + t : b * PACK + t + 1],
            )

        whole = slice(0, GROUP)
        left, right = slice(0, GROUP // 2), slice(GROUP // 2, GROUP)

        banks = h_banks()
        for a in range(KP):
            nc.vector.tensor_copy(out=v_code[a][:], in_=tab[a][:].indirect(idx_list[:]))
            tiles = w1_tiles(0, a)
            if a < KP - 1:
                round_w1(w1_raw[0, a], tiles[0], whole, True)
                quantise_w1(tiles, 0, PACK - 1)
            else:
                round_w1(w1_raw[0, a], tiles[0], left, True)
                round_w1(w1_raw[0, a], tiles[0], right, False)
                for t in range(PACK):
                    quantise_w1(tiles, t, t)
            for t in range(PACK):
                first_pass(a, t, tiles, banks)

        w4_code = keep.tile([P, RB, 2 * N], U8, name="w4_code", tag="big0", align_bytes=64)
        w4_scale = keep.tile([P, RB, N], U8, name="w4_scale", tag="big1", align_bytes=64)
        for b in range(RB):
            nc.vector.tensor_copy(
                out=w4_code[:, b, :].rearrange("p (t q e) -> p t q e", t=PACK, e=2),
                in_=w4_raw[:, b, :].rearrange("p (q t e) -> p t q e", t=PACK, e=2),
            )
        nc.vector.tensor_copy(
            out=w4_scale[:].rearrange("p b (t q) -> p b t q", t=PACK),
            in_=w4_scale_raw[:].rearrange("p b (q t) -> p b t q", t=PACK),
        )

        for a in range(KP):
            w1_raw[1, a] = load_w1(1, a, 1)
        mix_t = []
        for b in range(RB):
            mt = ring.tile([P, PACK, M], F32, name=f"mix{b}", tag="rows")
            nc.sync.dma_start(out=mt[:], in_=mix[b * GROUP : (b + 1) * GROUP, :].rearrange("(p t) m -> p t m", t=PACK))
            mix_t.append(mt)

        def look_exp(b, t, h, bias, out, offsets):
            col = b * PACK + t
            nc.scalar.activation(
                out=out, in_=h[:].indirect(offsets), func=ACT.Exp,
                bias=bias[:, t : t + 1], scale=row_consts["temp"][:, col : col + 1],
            )

        def look_gate(b, t, h, out):
            col = b * PACK + t
            nc.scalar.activation(
                out=out, in_=h[:].indirect(p2_list[:]), func=ACT.Sigmoid,
                bias=row_consts["thr"][:, col : col + 1], scale=row_consts["steep"][:, col : col + 1],
            )

        neg_temp = keep.tile([P, RB * PACK], F32, name="neg_temp")
        nc.vector.tensor_scalar(neg_temp[:], row_consts["temp"][:], -1.0, None, ALU.mult)
        tops = keep.tile([P, 2, RB * PACK], F32, name="tops")
        h = {(b, t): keep.tile([P, S], F32, name=f"h{b}{t}") for b in range(RB) for t in range(PACK)}
        later = [w1_tiles(1, a) for a in range(KP)]
        bias0 = keep.tile([P, PACK], F32, name="bias0", tag="gate0")
        a0 = ring.tile([P, PACK, M], F32, name="a0", tag="rows")

        def first_look(t):
            nc.vector.tensor_scalar(
                bias0[:, t : t + 1], tops[:, 0, t : t + 1], tops[:, 1, t : t + 1], neg_temp[:, t : t + 1],
                ALU.max, ALU.mult,
            )
            look_exp(0, t, h[0, t], bias0, a0[:, t, :], p1_list[:])

        round_w1(w1_raw[1, 0], later[0][0], whole, True)
        for t in range(PACK):
            empty_bank(0, t, 0, banks)
            if t > 0:
                first_look(t - 1)
            empty_bank(0, t, 1, banks)
            if t == PACK - 2:
                quantise_w1(later[0], 0, PACK - 1)
        first_look(PACK - 1)

        banks = h_banks()
        for t in range(PACK):
            first_pass(0, t, later[0], banks)
        for a in range(1, KP):
            round_w1(w1_raw[1, a], later[a][0], whole, False)
        for t in range(PACK):
            for a in range(1, KP):
                quantise_w1(later[a], t, t)
        for t in range(PACK):
            for a in range(1, KP):
                first_pass(a, t, later[a], banks)

        tenor_rows = tenor.rearrange("(p t) m -> p t m", t=PACK)
        tenor_t = []
        for hf in range(2):
            tt = keep.tile([P, PACK, HALF], F32, name=f"tenor{hf}", tag=f"dealt{hf}", align_bytes=64)
            nc.sync.dma_start(out=tt[:], in_=tenor_rows[:, :, hf * HALF : (hf + 1) * HALF])
            tenor_t.append(tt)

        c0 = keep.tile([P, PACK, M], F32, name="c0", tag="gate0")
        for t in range(PACK):
            look_gate(0, t, h[0, t], c0[:, t, :])
        c1 = keep.tile([P, PACK, M], F32, name="c1", tag="big2", align_bytes=64)
        for t in range(PACK):
            for hf in range(S // BANK):
                empty_bank(1, t, hf, banks)
            look_gate(1, t, h[1, t], c1[:, t, :])
        top1 = keep.tile([P, PACK], F32, name="top1")
        bias1 = keep.tile([P, PACK], F32, name="bias1")
        nc.vector.tensor_tensor(top1[:], tops[:, 0, PACK : 2 * PACK], tops[:, 1, PACK : 2 * PACK], ALU.max)
        nc.vector.tensor_tensor(bias1[:], top1[:], neg_temp[:, PACK : 2 * PACK], ALU.mult)
        a1 = ring.tile([P, 2, PACK, HALF], F32, name="a1", tag="rows")
        for hf in range(2):
            for t in range(PACK):
                look_exp(1, t, h[1, t], bias1, a1[:, hf, t, :], p1_list[:, hf * HALF // 16 : (hf + 1) * HALF // 16])

        def factor(b, c):
            fac = keep.tile([P, PACK, M], F32, name=f"fac{b}", tag=("dealt2" if b == 0 else "w1_code02"), align_bytes=64)
            if b == 0:
                for t in range(PACK):
                    nc.gpsimd.tensor_tensor(fac[:, t, :], c[:, t, :], mix_t[b][:, t, :], ALU.mult)
            else:
                for t in range(0, PACK, 2):
                    nc.vector.tensor_tensor(fac[:, t : t + 2, :], c[:, t : t + 2, :], mix_t[b][:, t : t + 2, :], ALU.mult)
            for t in range(PACK):
                col = b * PACK + t
                nc.vector.tensor_scalar(
                    fac[:, t, :], fac[:, t, :], row_consts["tilt"][:, col : col + 1], None, ALU.add
                )
            return fac

        def woven(flat):
            return flat.rearrange("p (c i t) -> p c t i", i=4, t=PACK)

        def by_lines(planes):
            return planes.rearrange("p t (c i) -> p c t i", i=4)

        def round_z(name, fac, a_part, width, tag):
            z_bf = keep.tile([P, PACK * width], BF16, name=f"z_bf{name}", tag=tag, align_bytes=64)
            nc.vector.tensor_tensor(woven(z_bf[:]), by_lines(fac), by_lines(a_part), ALU.mult)
            return z_bf

        def quantise_z(name, z_bf, width):
            code = keep.tile([P, width], U32, name=f"z_code{name}", align_bytes=64)
            scale = keep.tile([P, width], U8, name=f"z_scale{name}", align_bytes=64)
            nc.vector.quantize_mx(out=code[:].bitcast(FP8X4), scales=scale[:], in_=z_bf)
            return code, scale

        y_banks = [psum.tile([P, PACK, QUARTER], F32, name=f"ybank{qd}", tag=f"bank{qd}0") for qd in range(4)]

        def second_pass(b, qd, code, scale):
            for t in range(PACK):
                nc.tensor.matmul_mx(
                    out=y_banks[qd][:, t, :],
                    lhsT=w4_code[:, b, 2 * P * t : 2 * P * (t + 1)].bitcast(FP4X4),
                    lhsT_scale=w4_scale[:, b, P * t : P * (t + 1)],
                    rhs=code.bitcast(FP8X4),
                    rhs_scale=scale,
                    start=(b == 0 and t == 0),
                    stop=(b == RB - 1 and t == PACK - 1),
                )

        def quarter(qd):
            return slice(qd * QUARTER, (qd + 1) * QUARTER)

        def half(hf):
            return slice(hf * HALF, (hf + 1) * HALF)

        def multiply_half(b, hf, z_bf):
            z_code, z_scale = quantise_z(f"{b}{hf}", z_bf[:], HALF)
            for s in range(2):
                second_pass(b, 2 * hf + s, z_code[:, quarter(s)], z_scale[:, quarter(s)])

        fac0 = factor(0, c0)
        z0 = [round_z(f"0{hf}", fac0[:, :, half(hf)], a0[:, :, half(hf)], HALF, f"z_bf0{hf}") for hf in range(2)]
        for hf in range(2):
            multiply_half(0, hf, z0[hf])
        fac1 = factor(1, c1)
        multiply_half(1, 0, round_z("10", fac1[:, :, half(0)], a1[:, 0], HALF, "z_bf10"))

        y_scale = keep.tile([P, M], U8, name="y_scale", align_bytes=64)
        out_rows = out_0.rearrange("(p t) m -> p t m", t=PACK)
        out_words = out_1[0].rearrange("p m t -> p (m t)")

        def finish(hf):
            cols = slice(hf * HALF, (hf + 1) * HALF)
            y = keep.tile([P, PACK, HALF], F32, name=f"y{hf}")
            y_bf = keep.tile([P, PACK * HALF], BF16, name=f"y_bf{hf}", align_bytes=64)
            for s in range(2):
                qd = 2 * hf + s
                nc.vector.tensor_tensor(y[:, :, quarter(s)], y_banks[qd][:], tenor_t[hf][:, :, quarter(s)], ALU.mult)
                dst = woven(y_bf[:, PACK * QUARTER * s : PACK * QUARTER * (s + 1)])
                if qd < 3:
                    nc.scalar.copy(out=dst, in_=by_lines(y[:, :, quarter(s)]))
                else:
                    nc.vector.tensor_copy(out=dst, in_=by_lines(y[:, :, quarter(s)]))
            nc.sync.dma_start(out=out_rows[:, :, cols], in_=y[:])
            return y_bf

        def planes(hf, y_bf):
            cols = slice(hf * HALF, (hf + 1) * HALF)
            y_code = keep.tile([P, HALF], U32, name=f"y_code{hf}", align_bytes=64)
            nc.vector.quantize_mx(out=y_code[:].bitcast(FP8X4), scales=y_scale[:, cols], in_=y_bf[:])
            nc.sync.dma_start(
                out=out_words[:, PACK * hf * HALF : PACK * (hf + 1) * HALF].bitcast(I32), in_=y_code[:].bitcast(I32)
            )

        y_bf0 = finish(0)
        last = keep.tile([P, PACK * HALF], BF16, name="z_bf_last", tag="dealt0", align_bytes=64)
        for s in range(2):
            nc.vector.tensor_tensor(
                woven(last[:, PACK * QUARTER * s : PACK * QUARTER * (s + 1)]),
                by_lines(fac1[:, :, quarter(2 + s)]), by_lines(a1[:, 1, :, quarter(s)]), ALU.mult,
            )
        for s in range(2):
            z_code, z_scale = quantise_z(f"q{s}", last[:, PACK * QUARTER * s : PACK * QUARTER * (s + 1)], QUARTER)
            second_pass(1, 2 + s, z_code[:], z_scale[:])
        planes(0, y_bf0)
        planes(1, finish(1))
        for quad in range(4):
            queue = nc.scalar if quad % 2 == 0 else nc.sync
            queue.dma_start(
                out=out_2[0, 4 * quad : 4 * quad + 4, :].bitcast(I32),
                in_=y_scale[32 * quad : 32 * quad + 4, :].bitcast(I32),
            )
